import numpy as np
import ml_dtypes


def mxq(x, axis, fmt="e4m3"):
    dtype, down = {"e4m3": (ml_dtypes.float8_e4m3fn, 7), "e5m2": (ml_dtypes.float8_e5m2, 14)}[fmt]
    v = np.moveaxis(np.asarray(x, np.float32).astype(ml_dtypes.bfloat16).astype(np.float64), axis, -1)
    blocks = v.reshape(v.shape[:-1] + (-1, 32))
    amax = np.abs(blocks).max(-1, keepdims=True)
    byte = np.maximum(np.where(amax > 0, np.frexp(amax)[1] - 1 + 127, 0) - down, 1)
    scale = np.exp2(byte - 127.0)
    codes = (blocks / scale).astype(np.float32).astype(dtype).astype(np.float64)
    return np.moveaxis((codes * scale).reshape(v.shape), -1, axis)


WIDE = False


def mx_kscale(k):
    if not WIDE:
        return np.ones(k)
    levels = np.array([10, -10, 5, -5, 0])
    if k % 512:
        return np.exp2(np.random.permutation(np.resize(levels, k // 32))).repeat(32)
    a = np.empty((k // 512, 16))
    for p in range(k // 512):
        a[p, :8] = np.random.permutation(np.resize(levels, 8))
        for g in range(8):
            far = levels[np.abs(levels - a[p, g]) >= 10]
            a[p, g + 8] = far[np.random.randint(len(far))]
    return np.exp2(a.ravel()).repeat(32)


def f64(x):
    return np.asarray(x).astype(np.float64)


def striped(idx):
    return np.tile(idx.reshape(-1, 16).T, (8, 1)).astype(np.uint16)


def unstriped(offs):
    return offs[:16].T.reshape(-1).astype(np.int64)


E2M1 = np.array([0.0, 0.5, 1.0, 1.5, 2.0, 3.0, 4.0, 6.0, -0.0, -0.5, -1.0, -1.5, -2.0, -3.0, -4.0, -6.0])


def pack_weight(w, fmt):
    k, n = w.shape
    w = f64(np.asarray(w, np.float32).astype(ml_dtypes.bfloat16)).reshape(k // 32, 32, n)
    amax = np.abs(w).max(1)
    if fmt == "e4m3":
        byte = np.frexp(amax)[1] - 1 + 127 - 7
    else:
        mant, ex = np.frexp(amax / 6.0)
        byte = np.where(mant > 0.5, ex, ex - 1) + 127
    byte = np.clip(np.where(amax > 0, byte, 1), 1, 254)
    scaled = (w * np.exp2(127.0 - byte)[:, None, :]).reshape(k, n).astype(np.float32)
    by_word = np.ascontiguousarray(scaled.reshape(k // 512, 128, 4, n).transpose(0, 1, 3, 2))
    if fmt == "e4m3":
        words = by_word.astype(ml_dtypes.float8_e4m3fn).view(np.uint8)
    else:
        c = by_word.astype(ml_dtypes.float4_e2m1fn).view(np.uint8) & 0xF
        words = (c[..., 0::2] | (c[..., 1::2] << 4)).reshape(k // 512, 128, 2 * n)
    return np.ascontiguousarray(words), np.ascontiguousarray(byte.astype(np.uint8).reshape(k // 512, 16, n))


def unpack_weight(words, scales, fmt):
    g, _, n = scales.shape
    words = np.ascontiguousarray(words).reshape(g, 128, n, -1)
    if fmt == "e4m3":
        vals = words.view(ml_dtypes.float8_e4m3fn).astype(np.float64)
    else:
        nib = np.empty((g, 128, n, 4), np.uint8)
        nib[..., 0::2] = words & 0xF
        nib[..., 1::2] = words >> 4
        vals = E2M1[nib]
    vals = vals * np.repeat(np.exp2(scales.astype(np.float64) - 127.0), 8, axis=1)[..., None]
    return vals.transpose(0, 1, 3, 2).reshape(g * 512, n)


def gelu(v):
    return 0.5 * v * (1.0 + np.tanh(np.sqrt(2.0 / np.pi) * (v + 0.044715 * v**3)))


def striped8(idx):
    return np.concatenate([v.reshape(-1, 16).T for v in idx]).astype(np.uint16)


def unstriped8(offs):
    return np.stack([offs[16 * g:16 * g + 16].T.reshape(-1) for g in range(8)]).astype(np.int64)


def runs(v, idx8):
    k = np.arange(v.shape[0])
    return v[k[:, None], idx8[k % 512 // 64]]


def bf(x):
    return np.asarray(x, np.float32).astype(ml_dtypes.bfloat16)


def planes(Y):
    n, m = Y.shape
    b = f64(bf(Y)).reshape(n // 32, 32, m)
    amax = np.abs(b).max(1)
    byte = np.clip(np.where(amax > 0, np.frexp(amax)[1] - 1 + 127 - 7, 1), 1, 254)
    codes = (b * np.exp2(127.0 - byte)[:, None, :]).reshape(n, m).astype(np.float32).astype(ml_dtypes.float8_e4m3fn).view(np.uint8)
    words = codes.reshape(n // 512, 128, 4, m).transpose(0, 1, 3, 2)
    return np.ascontiguousarray(words), np.ascontiguousarray(byte.astype(np.uint8).reshape(n // 512, 16, m))


K, H, T, S, P = 1024, 1024, 2048, 1024, 512

def setup_inputs():
    n = np.random.standard_normal
    s = mx_kscale(K)[:, None]
    u = mx_kscale(H)[:, None]
    d = {}
    d["tab_words"], d["tab_scales"] = pack_weight(n((K, T)) * s, "e4m3")
    d["offs"] = striped8(np.stack([np.random.permutation(T)[:S] for _ in range(8)]))
    d["pos1"] = striped(np.random.permutation(S)[:P])
    d["pos2"] = striped(np.random.permutation(S)[:P])
    d["w1"] = (0.8 * n((K, H)) / s / K ** 0.5).astype(np.float32)
    d["w2_words"], d["w2_scales"] = pack_weight(n((K, H)) / s / K ** 0.5, "e2m1")
    d["crust"] = (0.7 * n((H, S))).astype(np.float32)
    d["gain"] = (np.exp(0.3 * n(H)) * u[:, 0]).astype(np.float32)
    d["w3"] = (n((H, H)) / u / H ** 0.5).astype(np.float32)
    d["size"] = np.exp(0.8 * n(H)).astype(np.float32)
    return d

def reference(tab_words, tab_scales, offs, pos1, pos2, w1, w2_words, w2_scales, crust, gain, w3, size):
    v = runs(unpack_weight(tab_words, tab_scales, "e4m3"), unstriped8(offs))
    w2 = unpack_weight(w2_words, w2_scales, "e2m1")
    plain = mxq(f64(w1), 0, "e4m3").T @ v
    crusted = w2.T @ v
    h = plain + f64(crust) * crusted
    face = np.tanh(h[:, unstriped(pos1)] - h[:, unstriped(pos2)])
    x = mxq(face * f64(gain)[:, None], 0, "e4m3")
    y = ((mxq(f64(w3), 0, "e4m3").T @ x) + face) * f64(size)[:, None]
    words, scales = planes(y)
    return y, words, scales

from contextlib import ExitStack

import concourse.mybir as mybir

K, H, T, S, NP = 1024, 1024, 2048, 1024, 512
FLOPS = 2 * K * H * S * 2 + 2 * H * H * NP

F32 = mybir.dt.float32
BF16 = mybir.dt.bfloat16
I32 = mybir.dt.int32
U32 = mybir.dt.uint32
U16 = mybir.dt.uint16
U8 = mybir.dt.uint8
FP8X4 = mybir.dt.float8_e4m3fn_x4
FP4X4 = mybir.dt.float4_e2m1fn_x4
MULT = mybir.AluOpType.mult
ADD = mybir.AluOpType.add
SUB = mybir.AluOpType.subtract
TANH = mybir.ActivationFunctionType.Tanh
COPY = mybir.ActivationFunctionType.Copy

P = 128
G = 512
HALF = 256


def tile_list_petal_corrosion_features_kernel(
    tc, tab_words, tab_scales, offs, pos1, pos2, w1, w2_words, w2_scales, crust, gain, w3, size, out_0, out_1, out_2
):
    nc = tc.nc
    with ExitStack() as ctx:
        keep = ctx.enter_context(tc.tile_pool(name="keep", bufs=1))
        ring = ctx.enter_context(tc.tile_pool(name="ring", bufs=2))
        psum = ctx.enter_context(tc.psum_pool(name="psum", bufs=8))

        offs_sb = keep.tile([P, S // 16], U16, name="offs_sb")
        pos1_sb = keep.tile([P, NP // 16], U16, name="pos1_sb")
        pos2_sb = keep.tile([P, NP // 16], U16, name="pos2_sb")
        tab_w = [keep.tile([P, T], I32, name="tab_w%d" % a, align_bytes=64) for a in range(2)]
        tab_s = keep.tile([P, T], U8, name="tab_s", align_bytes=64)
        picked_s = keep.tile([P, S], U8, name="picked_s", align_bytes=64)
        v_s = [keep.tile([P, S], U8, name="v_s%d" % a, align_bytes=64) for a in range(2)]
        v_w = {(a, c): keep.tile([P, G], U32, name="v_w%d%d" % (a, c), align_bytes=64) for a in range(2) for c in range(2)}
        w2_raw = keep.tile([P, 2, 2 * H], U8, name="w2_raw", align_bytes=64)
        w2_w = [keep.tile([P, 2 * H], U8, name="w2_w%d" % a, align_bytes=64) for a in range(2)]
        w2_sraw = keep.tile([P, 2, H], U8, name="w2_sraw", align_bytes=64)
        w2_s = keep.tile([P, 2, H], U8, name="w2_s", align_bytes=64)
        gain_sb = keep.tile([P, 2, 4], F32, name="gain_sb")
        size_sb = keep.tile([P, 2, 4], F32, name="size_sb")
        h = [keep.tile([P, S], F32, name="h%d" % i, align_bytes=64) for i in range(8)]
        raw = {}
        codes = {}
        scales = {}
        for wn in ("w1", "w3"):
            for b in range(2):
                for a in range(2):
                    raw[wn, b, a] = keep.tile([P, 4, G], F32, name="raw_%s_%d%d" % (wn, b, a), align_bytes=64)
                    codes[wn, b, a] = keep.tile([P, G], U32, name="codes_%s_%d%d" % (wn, b, a), align_bytes=64)
                    scales[wn, b, a] = keep.tile([P, G], U8, name="scales_%s_%d%d" % (wn, b, a), align_bytes=64)
        x_rows = [keep.tile([P, 2, 4, HALF], BF16, name="x_rows%d" % b, align_bytes=64) for b in range(2)]
        y = [keep.tile([P, 2, 4, HALF], F32, name="y%d" % b, align_bytes=64) for b in range(2)]
        x_w = {(b, c): keep.tile([P, HALF], U32, name="x_w%d%d" % (b, c), align_bytes=64) for b in range(2) for c in range(2)}
        x_s = {(b, c): keep.tile([P, HALF], U8, name="x_s%d%d" % (b, c), align_bytes=64) for b in range(2) for c in range(2)}
        y_w = {(b, c): keep.tile([P, HALF], U32, name="y_w%d%d" % (b, c), align_bytes=64) for b in range(2) for c in range(2)}
        y_s = keep.tile([P, 2, NP], U8, name="y_s", align_bytes=64)

        nc.vector.memset(tab_s[:].bitcast(I32), 0)
        nc.gpsimd.memset(w2_sraw[:].rearrange("p a n -> p (a n)").bitcast(I32), 0)
        for a in range(2):
            nc.vector.memset(v_s[a][:].bitcast(I32), 0)

        nc.sync.dma_start(offs_sb[:], offs)
        for a in range(2):
            for e in range(2):
                nc.scalar.dma_start(
                    tab_s[:].bitcast(I32)[2 * a + e : P : 16, :],
                    tab_scales[a].rearrange("(g e) n -> e g n", e=2)[e].bitcast(I32),
                )
        for a in range(2):
            nc.sync.dma_start(tab_w[a][:], tab_words[a].rearrange("p n t -> p (n t)").bitcast(I32))
        nc.sync.dma_start(w2_raw[:].bitcast(I32), w2_words.rearrange("a p n -> p a n").bitcast(I32))
        for q in range(4):
            nc.gpsimd.dma_start(
                w2_sraw[:].bitcast(I32)[32 * q : 32 * q + 4, :, :],
                w2_scales[:, 4 * q : 4 * q + 4, :].rearrange("a r n -> r a n").bitcast(I32),
            )

        def load_crust(i):
            nc.sync.dma_start(h[i][:], crust.rearrange("(b p t) j -> b t p j", b=2, t=4)[i // 4, i % 4])

        def load_weight(wn, w, b, a):
            nc.sync.dma_start(
                raw[wn, b, a][:], w[G * a : G * (a + 1), G * b : G * (b + 1)].rearrange("(p j) c -> p j c", j=4)
            )

        load_weight("w1", w1, 0, 0)
        load_weight("w1", w1, 0, 1)
        load_crust(0)
        load_crust(1)
        nc.sync.dma_start(pos2_sb[:], pos2)
        nc.sync.dma_start(pos1_sb[:], pos1)
        load_crust(2)
        nc.sync.dma_start(gain_sb[:], gain.rearrange("(b p t) -> p b t", b=2, t=4))
        nc.sync.dma_start(size_sb[:], size.rearrange("(b p t) -> p b t", b=2, t=4))
        load_crust(3)
        load_weight("w1", w1, 1, 0)
        load_weight("w1", w1, 1, 1)
        for i in range(4, 8):
            load_crust(i)
            load_weight("w3", w3, (i - 4) // 2, i % 2)

        nc.vector.tensor_copy(picked_s[:], tab_s[:].indirect(offs_sb[:]))
        for a in range(2):
            for odd in range(2):
                for e in range(2):
                    (nc.scalar if a == 0 else nc.gpsimd).dma_start(
                        v_s[a][:].bitcast(I32)[2 * odd + e : P : 32, :],
                        picked_s[:].bitcast(I32)[16 * odd + 2 * a + e : P : 32, :],
                    )

        def pick_words(a, c):
            nc.vector.tensor_copy(v_w[a, c][:], tab_w[a][:].bitcast(U32).indirect(offs_sb[:, 32 * c : 32 * (c + 1)]))

        nc.vector.tensor_copy(
            w2_s[:].rearrange("p a (b t m) -> p a b t m", b=2, t=4),
            w2_sraw[:].rearrange("p a (b m t) -> p a b t m", b=2, t=4),
        )
        pick_words(0, 0)
        pick_words(0, 1)
        pick_words(1, 0)
        for a in range(2):
            nc.vector.tensor_copy(
                w2_w[a][:].bitcast(U16).rearrange("p (b t m) -> p b t m", b=2, t=4),
                w2_raw[:, a, :].bitcast(U16).rearrange("p (b m t) -> p b t m", b=2, t=4),
            )
        pick_words(1, 1)

        rounded = {}

        def round_weight(wn, b, a):
            wb = ring.tile([P, 4 * G], BF16, name="w_bf", align_bytes=64)
            nc.scalar.copy(
                wb[:].rearrange("p (t m j) -> p m j t", t=4, j=4),
                raw[wn, b, a][:].rearrange("p j (m t) -> p m j t", t=4),
            )
            rounded[wn, b, a] = wb

        def quantize_weight(wn, b, a):
            nc.vector.quantize_mx(out=codes[wn, b, a][:].bitcast(FP8X4), scales=scales[wn, b, a][:], in_=rounded[wn, b, a][:])

        def crusted_product(i, c):
            b, t = divmod(i, 4)
            bank = psum.tile([P, G], F32, name="bank")
            for a in range(2):
                col = G * b + P * t
                nc.tensor.matmul_mx(
                    out=bank[:],
                    lhsT=w2_w[a][:, 2 * col : 2 * (col + P)].bitcast(FP4X4),
                    lhsT_scale=w2_s[:, a, col : col + P],
                    rhs=v_w[a, c][:].bitcast(FP8X4),
                    rhs_scale=v_s[a][:, G * c : G * (c + 1)],
                    start=(a == 0),
                    stop=(a == 1),
                )
            cols = h[i][:, G * c : G * (c + 1)]
            nc.vector.tensor_tensor(cols, bank[:], cols, MULT)

        def plain_product(i, c):
            b, t = divmod(i, 4)
            bank = psum.tile([P, G], F32, name="bank")
            for a in range(2):
                nc.tensor.matmul_mx(
                    out=bank[:],
                    lhsT=codes["w1", b, a][:, P * t : P * (t + 1)].bitcast(FP8X4),
                    lhsT_scale=scales["w1", b, a][:, P * t : P * (t + 1)],
                    rhs=v_w[a, c][:].bitcast(FP8X4),
                    rhs_scale=v_s[a][:, G * c : G * (c + 1)],
                    start=(a == 0),
                    stop=(a == 1),
                )
            cols = h[i][:, G * c : G * (c + 1)]
            nc.vector.tensor_tensor(cols, bank[:], cols, ADD)

        outer = {}

        def pick_outer(i, c0, c1):
            n = HALF * (c1 - c0)
            g = ring.tile([P, n], F32, name="outer")
            nc.vector.tensor_copy(g[:], h[i][:].indirect(pos2_sb[:, 16 * c0 : 16 * c1]))
            outer[i] = g

        def contrast(i, c0, c1):
            b, t = divmod(i, 4)
            n = HALF * (c1 - c0)
            d = ring.tile([P, n], F32, name="diff")
            nc.vector.tensor_tensor(d[:], h[i][:].indirect(pos1_sb[:, 16 * c0 : 16 * c1]), outer[i][:], SUB)
            face = ring.tile([P, n], F32, name="face")
            nc.scalar.activation(face[:], d[:], TANH)
            fv = face[:].rearrange("p (c j) -> p c j", j=HALF)
            nc.scalar.activation(x_rows[b][:, c0:c1, t, :], fv, COPY, scale=gain_sb[:, b, t : t + 1])
            nc.scalar.activation(y[b][:, c0:c1, t, :], fv, COPY, scale=size_sb[:, b, t : t + 1])

        woven = {}

        def weave(key, rows):
            wv = ring.tile([P, 4 * HALF], BF16, name="woven", align_bytes=64, bufs=3)
            nc.scalar.copy(
                wv[:].rearrange("p (u i t) -> p u t i", i=4, t=4),
                rows.rearrange("p t (u i) -> p u t i", i=4),
            )
            woven[key] = wv

        def quantize_x(b, c):
            nc.vector.quantize_mx(out=x_w[b, c][:].bitcast(FP8X4), scales=x_s[b, c][:], in_=woven["x", b, c][:])

        def treat(i, c):
            b, t = divmod(i, 4)
            bank = psum.tile([P, G], F32, name="bank")
            for a in range(2):
                nc.tensor.matmul_mx(
                    out=bank[:, 0:HALF],
                    lhsT=codes["w3", b, a][:, P * t : P * (t + 1)].bitcast(FP8X4),
                    lhsT_scale=scales["w3", b, a][:, P * t : P * (t + 1)],
                    rhs=x_w[a, c][:].bitcast(FP8X4),
                    rhs_scale=x_s[a, c][:],
                    start=(a == 0),
                    stop=(a == 1),
                )
            rows = y[b][:, c, t, :]
            nc.vector.scalar_tensor_tensor(rows, bank[:, 0:HALF], size_sb[:, b, t : t + 1], rows, MULT, ADD)

        def store_y(b, c):
            nc.sync.dma_start(
                out_0[G * b : G * (b + 1), HALF * c : HALF * (c + 1)].rearrange("(p t) j -> p t j", t=4), y[b][:, c, :, :]
            )
            weave(("y", b, c), y[b][:, c, :, :])

        def quantize_y(b, c):
            nc.vector.quantize_mx(
                out=y_w[b, c][:].bitcast(FP8X4), scales=y_s[:, b, HALF * c : HALF * (c + 1)], in_=woven["y", b, c][:]
            )
            nc.sync.dma_start(
                out_1[b].rearrange("p m t -> p (m t)").bitcast(I32)[:, HALF * c : HALF * (c + 1)], y_w[b, c][:].bitcast(I32)
            )

        round_weight("w1", 0, 0)
        crusted_product(0, 0)
        crusted_product(0, 1)
        quantize_weight("w1", 0, 0)
        round_weight("w1", 0, 1)
        crusted_product(1, 0)
        crusted_product(1, 1)
        quantize_weight("w1", 0, 1)
        plain_product(0, 0)
        plain_product(0, 1)

        later = [("w1", 1, 0), ("w1", 1, 1), ("w3", 0, 0), ("w3", 0, 1), ("w3", 1, 0), ("w3", 1, 1)]
        for i in range(8):
            width = 2 if i < 4 else 1
            if i < len(later):
                round_weight(*later[i])
            if i + 1 < 8:
                plain_product(i + 1, 0)
            pick_outer(i, 0, width)
            if i + 1 < 8:
                plain_product(i + 1, 1)
            contrast(i, 0, width)
            if i + 2 < 8:
                crusted_product(i + 2, 0)
            if i < len(later):
                quantize_weight(*later[i])
            if i + 2 < 8:
                crusted_product(i + 2, 1)
            if i == 3:
                weave(("x", 0, 0), x_rows[0][:, 0, :, :])
                weave(("x", 0, 1), x_rows[0][:, 1, :, :])
            if i == 5:
                quantize_x(0, 0)
                quantize_x(0, 1)
        weave(("x", 1, 0), x_rows[1][:, 0, :, :])
        for i in range(4, 8):
            pick_outer(i, 1, 2)
            if i == 6:
                quantize_x(1, 0)
            contrast(i, 1, 2)
        weave(("x", 1, 1), x_rows[1][:, 1, :, :])
        for i in range(8):
            treat(i, 0)
            if i == 3:
                store_y(0, 0)
            if i == 5:
                quantize_x(1, 1)
        store_y(1, 0)
        for i in range(8):
            treat(i, 1)
            if i == 1:
                quantize_y(0, 0)
            if i == 3:
                store_y(0, 1)
            if i == 5:
                quantize_y(1, 0)
        store_y(1, 1)
        quantize_y(0, 1)
        quantize_y(1, 1)
        for q in range(4):
            nc.scalar.dma_start(
                out_2[:, 4 * q : 4 * q + 4, :].rearrange("b r m -> r b m").bitcast(I32),
                y_s[:].bitcast(I32)[32 * q : 32 * q + 4, :, :],
            )
